import numpy as np
import ml_dtypes


def mxq(x, axis, fmt="e4m3"):
    dtype, down = {"e4m3": (ml_dtypes.float8_e4m3fn, 7), "e5m2": (ml_dtypes.float8_e5m2, 14)}[fmt]
    v = np.moveaxis(np.asarray(x, np.float32).astype(ml_dtypes.bfloat16).astype(np.float64), axis, -1)
    blocks = v.reshape(v.shape[:-1] + (-1, 32))
    amax = np.abs(blocks).max(-1, keepdims=True)
    byte = np.maximum(np.where(amax > 0, np.frexp(amax)[1] - 1 + 127, 0) - down, 1)
    scale = np.exp2(byte - 127.0)
    codes = (blocks / scale).astype(np.float32).astype(dtype).astype(np.float64)
    return np.moveaxis((codes * scale).reshape(v.shape), -1, axis)


WIDE = False


def mx_kscale(k):
    if not WIDE:
        return np.ones(k)
    levels = np.array([24, -24, 12, -12, 0])
    if k % 512:
        return np.exp2(np.random.permutation(np.resize(levels, k // 32))).repeat(32)
    a = np.empty((k // 512, 16))
    for p in range(k // 512):
        a[p, :8] = np.random.permutation(np.resize(levels, 8))
        for g in range(8):
            far = levels[np.abs(levels - a[p, g]) >= 10]
            a[p, g + 8] = far[np.random.randint(len(far))]
    return np.exp2(a.ravel()).repeat(32)


def f64(x):
    return np.asarray(x).astype(np.float64)


E2M1 = np.array([0.0, 0.5, 1.0, 1.5, 2.0, 3.0, 4.0, 6.0, -0.0, -0.5, -1.0, -1.5, -2.0, -3.0, -4.0, -6.0])


def pack_weight(w, fmt):
    k, n = w.shape
    w = f64(np.asarray(w, np.float32).astype(ml_dtypes.bfloat16)).reshape(k // 32, 32, n)
    amax = np.abs(w).max(1)
    if fmt == "e4m3":
        byte = np.frexp(amax)[1] - 1 + 127 - 7
    else:
        mant, ex = np.frexp(amax / 6.0)
        byte = np.where(mant > 0.5, ex, ex - 1) + 127
    byte = np.clip(np.where(amax > 0, byte, 1), 1, 254)
    scaled = (w * np.exp2(127.0 - byte)[:, None, :]).reshape(k, n).astype(np.float32)
    by_word = np.ascontiguousarray(scaled.reshape(k // 512, 128, 4, n).transpose(0, 1, 3, 2))
    if fmt == "e4m3":
        words = by_word.astype(ml_dtypes.float8_e4m3fn).view(np.uint8)
    else:
        c = by_word.astype(ml_dtypes.float4_e2m1fn).view(np.uint8) & 0xF
        words = (c[..., 0::2] | (c[..., 1::2] << 4)).reshape(k // 512, 128, 2 * n)
    return np.ascontiguousarray(words), np.ascontiguousarray(byte.astype(np.uint8).reshape(k // 512, 16, n))


def unpack_weight(words, scales, fmt):
    g, _, n = scales.shape
    words = np.ascontiguousarray(words).reshape(g, 128, n, -1)
    if fmt == "e4m3":
        vals = words.view(ml_dtypes.float8_e4m3fn).astype(np.float64)
    else:
        nib = np.empty((g, 128, n, 4), np.uint8)
        nib[..., 0::2] = words & 0xF
        nib[..., 1::2] = words >> 4
        vals = E2M1[nib]
    vals = vals * np.repeat(np.exp2(scales.astype(np.float64) - 127.0), 8, axis=1)[..., None]
    return vals.transpose(0, 1, 3, 2).reshape(g * 512, n)


def planes(y):
    n, m = y.shape
    v = y.astype(np.float32).astype(ml_dtypes.bfloat16).astype(np.float64).reshape(n // 32, 32, m)
    top = np.abs(v).max(1)
    byte = np.clip(np.where(top > 0, np.frexp(top)[1] - 1 + 127 - 7, 1), 1, 254)
    codes = (v * np.exp2(127.0 - byte)[:, None, :]).reshape(n, m).astype(np.float32).astype(ml_dtypes.float8_e4m3fn).view(np.uint8)
    words = codes.reshape(n // 512, 128, 4, m).transpose(0, 1, 3, 2)
    return np.ascontiguousarray(words), np.ascontiguousarray(byte.astype(np.uint8).reshape(n // 512, 16, m))


K, R, M, N, T = 2048, 512, 512, 512, 512


def setup_inputs():
    n = np.random.standard_normal
    u = mx_kscale(R)[:, None]
    s = mx_kscale(K)[:, None]
    p_w8 = pack_weight(n((K, R)) / np.sqrt(K) / s * u.T, "e4m3")
    return {
        "x": (n((K, T)) * s).astype(np.float32),
        "w8_words": p_w8[0],
        "w8_scales": p_w8[1],
        "wk": (n((R, M)) / np.sqrt(R) / u).astype(np.float32),
        "wv": (n((R, N)) / np.sqrt(R) / u).astype(np.float32),
    }


def reference(x, w8_words, w8_scales, wk, wv):
    x_ = mxq(f64(x), 0, "e4m3")
    w8_ = unpack_weight(w8_words, w8_scales, "e4m3")
    c = w8_.T @ x_
    c_ = mxq(c, 0, "e4m3")
    wk_ = mxq(f64(wk), 0, "e4m3")
    wv_ = mxq(f64(wv), 0, "e4m3")
    kk = wk_.T @ c_
    vv = wv_.T @ c_
    return (kk, vv, c) + planes(c)

@@ -1,0 +1,209 @@
+from contextlib import ExitStack
+
+import concourse.mybir as mybir
+
+K, R, M, N, T = 2048, 512, 512, 512, 512
+FLOPS = 2 * K * R * T + 2 * R * M * T + 2 * R * N * T
+
+F32 = mybir.dt.float32
+BF16 = mybir.dt.bfloat16
+I32 = mybir.dt.int32
+U8 = mybir.dt.uint8
+FP8X4 = mybir.dt.float8_e4m3fn_x4
+
+P = 128
+PACK = 4
+K_PASS = P * PACK
+PASSES = K // K_PASS
+QUARTER = T // 4
+HALF = T // 2
+
+
+def tile_mix_mla_kernel(
+    tc, x, w8_words, w8_scales, wk, wv, out_0, out_1, out_2, out_3, out_4
+):
+    nc = tc.nc
+    with ExitStack() as ctx:
+        sb = ctx.enter_context(tc.tile_pool(name="sb", bufs=1))
+        ps = ctx.enter_context(tc.psum_pool(name="ps", bufs=1))
+        ctx.enter_context(tc.manual_schedule())
+
+        def sbuf(name, shape, dtype):
+            return sb.tile(shape, dtype, name=name, align_bytes=64)
+
+        def copy_on(engine, out, in_):
+            if engine == "vector":
+                nc.vector.tensor_copy(out=out, in_=in_)
+            else:
+                nc.scalar.copy(out=out, in_=in_)
+
+        def interleave(engine, grouped, rows):
+            copy_on(
+                engine,
+                grouped.rearrange("p (c i) j -> p c j i", i=4),
+                rows.rearrange("p j (c i) -> p c j i", i=4),
+            )
+
+        def quantize(codes, scales, grouped):
+            nc.vector.quantize_mx(
+                out=codes.bitcast(FP8X4),
+                scales=scales,
+                in_=grouped.rearrange("p c j -> p (c j)"),
+            )
+
+        banks = [ps.tile([P, PACK, QUARTER], F32, name="bank%d" % b) for b in range(8)]
+
+        w_raw = sbuf("w_raw", [P, PASSES, R], I32)
+        ws_raw = sbuf("ws_raw", [P, R], U8)
+        x_raw = [sbuf("x_raw%d" % a, [P, PACK, T], F32) for a in range(PASSES)]
+        wk_raw = sbuf("wk_raw", [P, PACK, M], F32)
+        wv_raw = sbuf("wv_raw", [P, PACK, N], F32)
+
+        nc.vector.memset(ws_raw[:].bitcast(I32), 0)
+        nc.sync.dma_start(out=w_raw[:], in_=w8_words.rearrange("a p r i -> p a (r i)").bitcast(I32))
+        for quad in range(4):
+            nc.sync.dma_start(
+                out=ws_raw[32 * quad : 32 * quad + 16, :].bitcast(I32),
+                in_=w8_scales[:, 4 * quad : 4 * quad + 4, :].bitcast(I32),
+            )
+        for a in range(PASSES):
+            nc.sync.dma_start(
+                out=x_raw[a][:],
+                in_=x[a * K_PASS : (a + 1) * K_PASS, :].rearrange("(p j) t -> p j t", j=PACK),
+            )
+        nc.sync.dma_start(out=wk_raw[:], in_=wk.rearrange("(p j) m -> p j m", j=PACK))
+        nc.sync.dma_start(out=wv_raw[:], in_=wv.rearrange("(p j) n -> p j n", j=PACK))
+
+        w_codes = [sbuf("w_codes%d" % a, [P, R], I32) for a in range(PASSES)]
+        w_scales = sbuf("w_scales", [P, R], U8)
+        for a in range(PASSES):
+            nc.vector.tensor_copy(
+                out=w_codes[a][:].rearrange("p (j b m) -> p b j m", j=PACK, m=4),
+                in_=w_raw[:, a, :].rearrange("p (b m j) -> p b j m", j=PACK, m=4),
+            )
+        nc.vector.tensor_copy(
+            out=w_scales[:].rearrange("p (j m) -> p j m", j=PACK),
+            in_=ws_raw[:].rearrange("p (m j) -> p j m", j=PACK),
+        )
+
+        x_grouped = [sbuf("x_grouped%d" % a, [P, T, PACK], BF16) for a in range(PASSES)]
+        x_codes = [sbuf("x_codes%d" % a, [P, T], I32) for a in range(PASSES)]
+        x_scales = [sbuf("x_scales%d" % a, [P, T], U8) for a in range(PASSES)]
+
+        def x_copy(engine, a, cols):
+            interleave(engine, x_grouped[a][:, cols, :], x_raw[a][:, :, cols])
+
+        def x_quantize(a, cols):
+            quantize(x_codes[a][:, cols], x_scales[a][:, cols], x_grouped[a][:, cols, :])
+
+        def quarter(q):
+            return slice(q * QUARTER, (q + 1) * QUARTER)
+
+        def half(h):
+            return slice(h * HALF, (h + 1) * HALF)
+
+        def down(a, q):
+            for j in range(PACK):
+                nc.tensor.matmul_mx(
+                    out=banks[q][:, j, :],
+                    lhsT=w_codes[a][:, j * P : (j + 1) * P].bitcast(FP8X4),
+                    lhsT_scale=w_scales[4 * a : P, j * P : (j + 1) * P],
+                    rhs=x_codes[a][:, quarter(q)].bitcast(FP8X4),
+                    rhs_scale=x_scales[a][:, quarter(q)],
+                    start=(a == 0 and j == 0),
+                    stop=(a == PASSES - 1 and j == PACK - 1),
+                )
+
+        for a in range(PASSES):
+            x_copy("vector", a, quarter(0))
+            x_copy("scalar", a, quarter(2))
+            x_copy("vector", a, quarter(1))
+            x_copy("scalar", a, quarter(3))
+            for q in range(4):
+                x_quantize(a, quarter(q))
+                down(a, q)
+
+        c_sb = sbuf("c_sb", [P, PACK, T], F32)
+        for q, engine in enumerate(("scalar", "vector", "scalar", "vector")):
+            copy_on(engine, c_sb[:, :, quarter(q)], banks[q][:])
+        nc.sync.dma_start(out=out_2.rearrange("(p j) t -> p j t", j=PACK), in_=c_sb[:])
+
+        c_grouped = sbuf("c_grouped", [P, T, PACK], BF16)
+        c_codes = sbuf("c_codes", [P, T], I32)
+        c_scales = sbuf("c_scales", [P, T], U8)
+        interleave("vector", c_grouped[:, half(0), :], c_sb[:, :, half(0)])
+        for q in (2, 3):
+            nc.scalar.copy(out=c_grouped[:, quarter(q), :], in_=banks[q][:].rearrange("p j t -> p t j"))
+
+        up_raw = (wk_raw, wv_raw)
+        up_out = (out_0, out_1)
+        up_grouped = [[sbuf("up_grouped%d%d" % (u, h), [P, HALF, PACK], BF16) for h in range(2)] for u in range(2)]
+        up_codes = [[sbuf("up_codes%d%d" % (u, h), [P, HALF], I32) for h in range(2)] for u in range(2)]
+        up_scales = [[sbuf("up_scales%d%d" % (u, h), [P, HALF], U8) for h in range(2)] for u in range(2)]
+        up_sb = [[sbuf("up_sb%d%d" % (u, h), [P, 2, T], F32) for h in range(2)] for u in range(2)]
+
+        def up_bank(u, h, e):
+            return banks[4 * (1 - u) + 2 * h + e][:].rearrange("p j t -> p (j t)")
+
+        def up_copy(engine, u, h):
+            copy_on(
+                engine,
+                up_grouped[u][h][:].rearrange("p (e b m) j -> p b j m e", e=2, m=2),
+                up_raw[u][:, :, half(h)].rearrange("p j (b m e) -> p b j m e", e=2, m=2),
+            )
+
+        def up_quantize(u, h):
+            quantize(up_codes[u][h][:], up_scales[u][h][:], up_grouped[u][h][:])
+
+        def up(u, h):
+            for e in range(2):
+                nc.tensor.matmul_mx(
+                    out=up_bank(u, h, e),
+                    lhsT=up_codes[u][h][:, e * P : (e + 1) * P].bitcast(FP8X4),
+                    lhsT_scale=up_scales[u][h][:, e * P : (e + 1) * P],
+                    rhs=c_codes[:].bitcast(FP8X4),
+                    rhs_scale=c_scales[:],
+                    start=True,
+                    stop=True,
+                )
+
+        def up_drain(engine, u, h, e):
+            copy_on(engine, up_sb[u][h][:, e, :], up_bank(u, h, e))
+
+        def up_store(u, h):
+            nc.sync.dma_start(
+                out=up_out[u][half(h), :].rearrange("(p e) t -> p e t", e=2), in_=up_sb[u][h][:]
+            )
+
+        up_copy("vector", 0, 0)
+        up_copy("scalar", 0, 1)
+        for h in range(2):
+            quantize(c_codes[:, half(h)], c_scales[:, half(h)], c_grouped[:, half(h), :])
+        nc.sync.dma_start(out=out_3[0].rearrange("p t i -> p (t i)").bitcast(I32), in_=c_codes[:])
+        for quad in range(4):
+            nc.sync.dma_start(
+                out=out_4[0, 4 * quad : 4 * quad + 4, :].bitcast(I32),
+                in_=c_scales[32 * quad : 32 * quad + 4, :].bitcast(I32),
+            )
+        for h in range(2):
+            up_quantize(0, h)
+            up(0, h)
+
+        up_copy("vector", 1, 0)
+        up_drain("scalar", 0, 0, 0)
+        up_drain("vector", 0, 0, 1)
+        up_store(0, 0)
+        up_quantize(1, 0)
+        up(1, 0)
+        up_drain("scalar", 0, 1, 0)
+        up_drain("scalar", 0, 1, 1)
+        up_store(0, 1)
+        up_copy("vector", 1, 1)
+        up_drain("scalar", 1, 0, 0)
+        up_drain("vector", 1, 0, 1)
+        up_store(1, 0)
+        up_quantize(1, 1)
+        up(1, 1)
+        up_drain("scalar", 1, 1, 0)
+        up_drain("vector", 1, 1, 1)
+        up_store(1, 1)

@@ -53,14 +53,17 @@ def tile_mix_mla_kernel(
 
         banks = [ps.tile([P, PACK, QUARTER], F32, name="bank%d" % b) for b in range(8)]
 
-        w_raw = sbuf("w_raw", [P, PASSES, R], I32)
+        w_early = sbuf("w_early", [P, PASSES - 1, R], I32)
+        w_last = sbuf("w_last", [P, R], I32)
+        w_raw = [w_early[:, a, :] for a in range(PASSES - 1)] + [w_last[:]]
+        w_words = w8_words.rearrange("a p r i -> p a (r i)").bitcast(I32)
         ws_raw = sbuf("ws_raw", [P, R], U8)
         x_raw = [sbuf("x_raw%d" % a, [P, PACK, T], F32) for a in range(PASSES)]
         wk_raw = sbuf("wk_raw", [P, PACK, M], F32)
         wv_raw = sbuf("wv_raw", [P, PACK, N], F32)
 
         nc.vector.memset(ws_raw[:].bitcast(I32), 0)
-        nc.sync.dma_start(out=w_raw[:], in_=w8_words.rearrange("a p r i -> p a (r i)").bitcast(I32))
+        nc.sync.dma_start(out=w_early[:], in_=w_words[:, 0 : PASSES - 1, :])
         for quad in range(4):
             nc.sync.dma_start(
                 out=ws_raw[32 * quad : 32 * quad + 16, :].bitcast(I32),
@@ -71,16 +74,21 @@ def tile_mix_mla_kernel(
                 out=x_raw[a][:],
                 in_=x[a * K_PASS : (a + 1) * K_PASS, :].rearrange("(p j) t -> p j t", j=PACK),
             )
+        nc.sync.dma_start(out=w_last[:], in_=w_words[:, PASSES - 1, :])
         nc.sync.dma_start(out=wk_raw[:], in_=wk.rearrange("(p j) m -> p j m", j=PACK))
         nc.sync.dma_start(out=wv_raw[:], in_=wv.rearrange("(p j) n -> p j n", j=PACK))
 
         w_codes = [sbuf("w_codes%d" % a, [P, R], I32) for a in range(PASSES)]
         w_scales = sbuf("w_scales", [P, R], U8)
-        for a in range(PASSES):
+
+        def w_deal(a):
             nc.vector.tensor_copy(
                 out=w_codes[a][:].rearrange("p (j b m) -> p b j m", j=PACK, m=4),
-                in_=w_raw[:, a, :].rearrange("p (b m j) -> p b j m", j=PACK, m=4),
+                in_=w_raw[a].rearrange("p (b m j) -> p b j m", j=PACK, m=4),
             )
+
+        for a in range(PASSES - 1):
+            w_deal(a)
         nc.vector.tensor_copy(
             out=w_scales[:].rearrange("p (j m) -> p j m", j=PACK),
             in_=ws_raw[:].rearrange("p (m j) -> p j m", j=PACK),
@@ -114,26 +122,47 @@ def tile_mix_mla_kernel(
                     stop=(a == PASSES - 1 and j == PACK - 1),
                 )
 
-        for a in range(PASSES):
-            x_copy("vector", a, quarter(0))
-            x_copy("scalar", a, quarter(2))
-            x_copy("vector", a, quarter(1))
-            x_copy("scalar", a, quarter(3))
-            for q in range(4):
-                x_quantize(a, quarter(q))
-                down(a, q)
-
         c_sb = sbuf("c_sb", [P, PACK, T], F32)
-        for q, engine in enumerate(("scalar", "vector", "scalar", "vector")):
-            copy_on(engine, c_sb[:, :, quarter(q)], banks[q][:])
-        nc.sync.dma_start(out=out_2.rearrange("(p j) t -> p j t", j=PACK), in_=c_sb[:])
-
         c_grouped = sbuf("c_grouped", [P, T, PACK], BF16)
         c_codes = sbuf("c_codes", [P, T], I32)
         c_scales = sbuf("c_scales", [P, T], U8)
-        interleave("vector", c_grouped[:, half(0), :], c_sb[:, :, half(0)])
-        for q in (2, 3):
-            nc.scalar.copy(out=c_grouped[:, quarter(q), :], in_=banks[q][:].rearrange("p j t -> p t j"))
+
+        def c_drain(engine, q):
+            copy_on(engine, c_sb[:, :, quarter(q)], banks[q][:])
+
+        def c_round_psum(engine, q):
+            copy_on(engine, c_grouped[:, quarter(q), :], banks[q][:].rearrange("p j t -> p t j"))
+
+        def c_round(engine, cols):
+            interleave(engine, c_grouped[:, cols, :], c_sb[:, :, cols])
+
+        def c_quantize(cols):
+            quantize(c_codes[:, cols], c_scales[:, cols], c_grouped[:, cols, :])
+
+        def c_store():
+            nc.sync.dma_start(out=out_2.rearrange("(p j) t -> p j t", j=PACK), in_=c_sb[:])
+
+        def codes_store():
+            nc.sync.dma_start(out=out_3[0].rearrange("p t i -> p (t i)").bitcast(I32), in_=c_codes[:])
+
+        def scales_store():
+            for quad in range(4):
+                nc.sync.dma_start(
+                    out=out_4[0, 4 * quad : 4 * quad + 4, :].bitcast(I32),
+                    in_=c_scales[32 * quad : 32 * quad + 4, :].bitcast(I32),
+                )
+
+        def warm(count):
+            for b in range(count):
+                nc.tensor.matmul_mx(
+                    out=banks[4 + b % 4][:].rearrange("p j t -> p (j t)"),
+                    lhsT=w_codes[0][:, 0:P].bitcast(FP8X4),
+                    lhsT_scale=w_scales[:, 0:P],
+                    rhs=x_codes[0][:].bitcast(FP8X4),
+                    rhs_scale=x_scales[0][:],
+                    start=True,
+                    stop=True,
+                )
 
         up_raw = (wk_raw, wv_raw)
         up_out = (out_0, out_1)
@@ -155,6 +184,23 @@ def tile_mix_mla_kernel(
         def up_quantize(u, h):
             quantize(up_codes[u][h][:], up_scales[u][h][:], up_grouped[u][h][:])
 
+        def up_columns(u, h, cols):
+            for e in range(2):
+                nc.tensor.matmul_mx(
+                    out=up_bank(u, h, e)[:, cols],
+                    lhsT=up_codes[u][h][:, e * P : (e + 1) * P].bitcast(FP8X4),
+                    lhsT_scale=up_scales[u][h][:, e * P : (e + 1) * P],
+                    rhs=c_codes[:, cols].bitcast(FP8X4),
+                    rhs_scale=c_scales[:, cols],
+                    start=True,
+                    stop=True,
+                )
+
+        def up_store_bank(u, h, e):
+            nc.sync.dma_start(
+                out=up_out[u][half(h), :].rearrange("(p e) t -> p e t", e=2)[:, e, :], in_=up_sb[u][h][:, e, :]
+            )
+
         def up(u, h):
             for e in range(2):
                 nc.tensor.matmul_mx(
@@ -175,35 +221,57 @@ def tile_mix_mla_kernel(
                 out=up_out[u][half(h), :].rearrange("(p e) t -> p e t", e=2), in_=up_sb[u][h][:]
             )
 
+        for a in range(3):
+            x_copy("vector", a, quarter(0))
+            x_copy("scalar", a, quarter(2))
+            x_copy("vector", a, quarter(1))
+            x_copy("scalar", a, quarter(3))
+            for q in range(4):
+                x_quantize(a, quarter(q))
+                down(a, q)
+        last = PASSES - 1
+        x_copy("vector", last, quarter(0))
+        x_copy("scalar", last, quarter(2))
+        x_copy("vector", last, quarter(1))
+        x_copy("scalar", last, quarter(3))
+        w_deal(last)
+        for q in range(4):
+            x_quantize(last, quarter(q))
+            down(last, q)
+        c_drain("scalar", 0)
+        c_drain("scalar", 1)
+        c_drain("vector", 2)
+        c_drain("scalar", 3)
+        c_store()
         up_copy("vector", 0, 0)
+        c_round("vector", half(0))
+        c_round_psum("scalar", 2)
+        c_round_psum("scalar", 3)
         up_copy("scalar", 0, 1)
-        for h in range(2):
-            quantize(c_codes[:, half(h)], c_scales[:, half(h)], c_grouped[:, half(h), :])
-        nc.sync.dma_start(out=out_3[0].rearrange("p t i -> p (t i)").bitcast(I32), in_=c_codes[:])
-        for quad in range(4):
-            nc.sync.dma_start(
-                out=out_4[0, 4 * quad : 4 * quad + 4, :].bitcast(I32),
-                in_=c_scales[32 * quad : 32 * quad + 4, :].bitcast(I32),
-            )
-        for h in range(2):
-            up_quantize(0, h)
-            up(0, h)
-
+        up_quantize(0, 0)
+        c_quantize(half(0))
+        up_columns(0, 0, half(0))
+        c_quantize(half(1))
+        up_columns(0, 0, half(1))
+        codes_store()
         up_copy("vector", 1, 0)
+        up_quantize(0, 1)
+        up(0, 1)
         up_drain("scalar", 0, 0, 0)
-        up_drain("vector", 0, 0, 1)
-        up_store(0, 0)
+        up_store_bank(0, 0, 0)
+        up_drain("scalar", 0, 0, 1)
+        up_store_bank(0, 0, 1)
+        up_copy("vector", 1, 1)
         up_quantize(1, 0)
         up(1, 0)
-        up_drain("scalar", 0, 1, 0)
-        up_drain("scalar", 0, 1, 1)
-        up_store(0, 1)
-        up_copy("vector", 1, 1)
-        up_drain("scalar", 1, 0, 0)
-        up_drain("vector", 1, 0, 1)
-        up_store(1, 0)
         up_quantize(1, 1)
         up(1, 1)
-        up_drain("scalar", 1, 1, 0)
-        up_drain("vector", 1, 1, 1)
-        up_store(1, 1)
+        up_drain("scalar", 0, 1, 0)
+        up_store_bank(0, 1, 0)
+        up_drain("vector", 0, 1, 1)
+        up_store_bank(0, 1, 1)
+        for h in range(2):
+            up_drain("scalar", 1, h, 0)
+            up_drain("vector", 1, h, 1)
+            up_store(1, h)
+        scales_store()

@@ -201,6 +201,18 @@ def tile_mix_mla_kernel(
                 out=up_out[u][half(h), :].rearrange("(p e) t -> p e t", e=2)[:, e, :], in_=up_sb[u][h][:, e, :]
             )
 
+        def upq(u, b, cols=slice(0, T)):
+            h, e = divmod(b, 2)
+            nc.tensor.matmul_mx(
+                out=up_bank(u, h, e)[:, cols],
+                lhsT=up_codes[u][h][:, e * P : (e + 1) * P].bitcast(FP8X4),
+                lhsT_scale=up_scales[u][h][:, e * P : (e + 1) * P],
+                rhs=c_codes[:, cols].bitcast(FP8X4),
+                rhs_scale=c_scales[:, cols],
+                start=True,
+                stop=True,
+            )
+
         def up(u, h):
             for e in range(2):
                 nc.tensor.matmul_mx(
@@ -250,10 +262,12 @@ def tile_mix_mla_kernel(
         up_copy("scalar", 0, 1)
         up_quantize(0, 0)
         c_quantize(half(0))
-        up_columns(0, 0, half(0))
+        upq(0,0,half(0))
         c_quantize(half(1))
-        up_columns(0, 0, half(1))
+        upq(0,0,half(1))
+        upq(0,1)
         codes_store()
+        scales_store()
         up_copy("vector", 1, 0)
         up_quantize(0, 1)
         up(0, 1)
@@ -274,4 +288,3 @@ def tile_mix_mla_kernel(
             up_drain("scalar", 1, h, 0)
             up_drain("vector", 1, h, 1)
             up_store(1, h)
-        scales_store()

@@ -81,10 +81,10 @@ def tile_mix_mla_kernel(
         w_codes = [sbuf("w_codes%d" % a, [P, R], I32) for a in range(PASSES)]
         w_scales = sbuf("w_scales", [P, R], U8)
 
-        def w_deal(a):
+        def w_deal(a, js=slice(0, PACK)):
             nc.vector.tensor_copy(
-                out=w_codes[a][:].rearrange("p (j b m) -> p b j m", j=PACK, m=4),
-                in_=w_raw[a].rearrange("p (b m j) -> p b j m", j=PACK, m=4),
+                out=w_codes[a][:].rearrange("p (j b m) -> p b j m", j=PACK, m=4)[:, :, js, :],
+                in_=w_raw[a].rearrange("p (b m j) -> p b j m", j=PACK, m=4)[:, :, js, :],
             )
 
         for a in range(PASSES - 1):
@@ -152,18 +152,6 @@ def tile_mix_mla_kernel(
                     in_=c_scales[32 * quad : 32 * quad + 4, :].bitcast(I32),
                 )
 
-        def warm(count):
-            for b in range(count):
-                nc.tensor.matmul_mx(
-                    out=banks[4 + b % 4][:].rearrange("p j t -> p (j t)"),
-                    lhsT=w_codes[0][:, 0:P].bitcast(FP8X4),
-                    lhsT_scale=w_scales[:, 0:P],
-                    rhs=x_codes[0][:].bitcast(FP8X4),
-                    rhs_scale=x_scales[0][:],
-                    start=True,
-                    stop=True,
-                )
-
         up_raw = (wk_raw, wv_raw)
         up_out = (out_0, out_1)
         up_grouped = [[sbuf("up_grouped%d%d" % (u, h), [P, HALF, PACK], BF16) for h in range(2)] for u in range(2)]
@@ -183,18 +171,6 @@ def tile_mix_mla_kernel(
 
         def up_quantize(u, h):
             quantize(up_codes[u][h][:], up_scales[u][h][:], up_grouped[u][h][:])
-
-        def up_columns(u, h, cols):
-            for e in range(2):
-                nc.tensor.matmul_mx(
-                    out=up_bank(u, h, e)[:, cols],
-                    lhsT=up_codes[u][h][:, e * P : (e + 1) * P].bitcast(FP8X4),
-                    lhsT_scale=up_scales[u][h][:, e * P : (e + 1) * P],
-                    rhs=c_codes[:, cols].bitcast(FP8X4),
-                    rhs_scale=c_scales[:, cols],
-                    start=True,
-                    stop=True,
-                )
 
         def up_store_bank(u, h, e):
             nc.sync.dma_start(
@@ -243,17 +219,24 @@ def tile_mix_mla_kernel(
                 down(a, q)
         last = PASSES - 1
         x_copy("vector", last, quarter(0))
-        x_copy("scalar", last, quarter(2))
-        x_copy("vector", last, quarter(1))
+        x_copy("scalar", last, quarter(1))
+        x_copy("vector", last, slice(256, 320))
         x_copy("scalar", last, quarter(3))
-        w_deal(last)
-        for q in range(4):
-            x_quantize(last, quarter(q))
-            down(last, q)
+        x_quantize(last, quarter(0))
+        w_deal(last, slice(0, 2))
+        w_deal(last, slice(2, 4))
+        down(last, 0)
+        x_quantize(last, quarter(1))
+        down(last, 1)
+        x_copy("vector", last, slice(320, 384))
+        x_quantize(last, quarter(3))
+        down(last, 3)
+        x_quantize(last, quarter(2))
+        down(last, 2)
         c_drain("scalar", 0)
-        c_drain("scalar", 1)
-        c_drain("vector", 2)
-        c_drain("scalar", 3)
+        c_drain("vector", 1)
+        c_drain("scalar", 2)
+        c_drain("vector", 3)
         c_store()
         up_copy("vector", 0, 0)
         c_round("vector", half(0))
@@ -262,29 +245,34 @@ def tile_mix_mla_kernel(
         up_copy("scalar", 0, 1)
         up_quantize(0, 0)
         c_quantize(half(0))
-        upq(0,0,half(0))
+        upq(0, 0, half(0))
         c_quantize(half(1))
-        upq(0,0,half(1))
-        upq(0,1)
+        upq(0, 0, half(1))
+        upq(0, 1)
         codes_store()
         scales_store()
         up_copy("vector", 1, 0)
         up_quantize(0, 1)
-        up(0, 1)
+        upq(0, 2)
+        upq(0, 3)
         up_drain("scalar", 0, 0, 0)
         up_store_bank(0, 0, 0)
         up_drain("scalar", 0, 0, 1)
         up_store_bank(0, 0, 1)
         up_copy("vector", 1, 1)
         up_quantize(1, 0)
-        up(1, 0)
+        upq(1, 0)
+        upq(1, 1)
         up_quantize(1, 1)
-        up(1, 1)
+        upq(1, 2)
+        upq(1, 3)
         up_drain("scalar", 0, 1, 0)
         up_store_bank(0, 1, 0)
         up_drain("vector", 0, 1, 1)
         up_store_bank(0, 1, 1)
-        for h in range(2):
-            up_drain("scalar", 1, h, 0)
-            up_drain("vector", 1, h, 1)
-            up_store(1, h)
+        up_drain("scalar", 1, 0, 0)
+        up_drain("vector", 1, 0, 1)
+        up_store(1, 0)
+        up_drain("scalar", 1, 1, 0)
+        up_drain("vector", 1, 1, 1)
+        up_store(1, 1)

@@ -17,6 +17,7 @@ K_PASS = P * PACK
 PASSES = K // K_PASS
 QUARTER = T // 4
 HALF = T // 2
+ALIGN = 256
 
 
 def tile_mix_mla_kernel(
@@ -29,7 +30,7 @@ def tile_mix_mla_kernel(
         ctx.enter_context(tc.manual_schedule())
 
         def sbuf(name, shape, dtype):
-            return sb.tile(shape, dtype, name=name, align_bytes=64)
+            return sb.tile(shape, dtype, name=name, align_bytes=ALIGN)
 
         def copy_on(engine, out, in_):
             if engine == "vector":
@@ -51,7 +52,15 @@ def tile_mix_mla_kernel(
                 in_=grouped.rearrange("p c j -> p (c j)"),
             )
 
-        banks = [ps.tile([P, PACK, QUARTER], F32, name="bank%d" % b) for b in range(8)]
+        def quarter(q):
+            return slice(q * QUARTER, (q + 1) * QUARTER)
+
+        def half(h):
+            return slice(h * HALF, (h + 1) * HALF)
+
+        whole = slice(0, T)
+
+        banks = [ps.tile([P, T], F32, name="bank%d" % b) for b in range(8)]
 
         w_early = sbuf("w_early", [P, PASSES - 1, R], I32)
         w_last = sbuf("w_last", [P, R], I32)
@@ -81,10 +90,10 @@ def tile_mix_mla_kernel(
         w_codes = [sbuf("w_codes%d" % a, [P, R], I32) for a in range(PASSES)]
         w_scales = sbuf("w_scales", [P, R], U8)
 
-        def w_deal(a, js=slice(0, PACK)):
+        def w_deal(a):
             nc.vector.tensor_copy(
-                out=w_codes[a][:].rearrange("p (j b m) -> p b j m", j=PACK, m=4)[:, :, js, :],
-                in_=w_raw[a].rearrange("p (b m j) -> p b j m", j=PACK, m=4)[:, :, js, :],
+                out=w_codes[a][:].rearrange("p (j b m) -> p b j m", j=PACK, m=4),
+                in_=w_raw[a].rearrange("p (b m j) -> p b j m", j=PACK, m=4),
             )
 
         for a in range(PASSES - 1):
@@ -104,22 +113,20 @@ def tile_mix_mla_kernel(
         def x_quantize(a, cols):
             quantize(x_codes[a][:, cols], x_scales[a][:, cols], x_grouped[a][:, cols, :])
 
-        def quarter(q):
-            return slice(q * QUARTER, (q + 1) * QUARTER)
+        def c_bank(h, pair):
+            return banks[2 * h + pair]
 
-        def half(h):
-            return slice(h * HALF, (h + 1) * HALF)
-
-        def down(a, q):
+        def down(a, h):
+            cols = half(h)
             for j in range(PACK):
                 nc.tensor.matmul_mx(
-                    out=banks[q][:, j, :],
+                    out=c_bank(h, j // 2)[:, half(j % 2)],
                     lhsT=w_codes[a][:, j * P : (j + 1) * P].bitcast(FP8X4),
                     lhsT_scale=w_scales[4 * a : P, j * P : (j + 1) * P],
-                    rhs=x_codes[a][:, quarter(q)].bitcast(FP8X4),
-                    rhs_scale=x_scales[a][:, quarter(q)],
-                    start=(a == 0 and j == 0),
-                    stop=(a == PASSES - 1 and j == PACK - 1),
+                    rhs=x_codes[a][:, cols].bitcast(FP8X4),
+                    rhs_scale=x_scales[a][:, cols],
+                    start=(a == 0 and j % 2 == 0),
+                    stop=(a == PASSES - 1 and j % 2 == 1),
                 )
 
         c_sb = sbuf("c_sb", [P, PACK, T], F32)
@@ -127,11 +134,12 @@ def tile_mix_mla_kernel(
         c_codes = sbuf("c_codes", [P, T], I32)
         c_scales = sbuf("c_scales", [P, T], U8)
 
-        def c_drain(engine, q):
-            copy_on(engine, c_sb[:, :, quarter(q)], banks[q][:])
-
-        def c_round_psum(engine, q):
-            copy_on(engine, c_grouped[:, quarter(q), :], banks[q][:].rearrange("p j t -> p t j"))
+        def c_drain(engine, h, pair):
+            copy_on(
+                engine,
+                c_sb[:, 2 * pair : 2 * pair + 2, half(h)],
+                c_bank(h, pair)[:].rearrange("p (j t) -> p j t", j=2),
+            )
 
         def c_round(engine, cols):
             interleave(engine, c_grouped[:, cols, :], c_sb[:, :, cols])
@@ -139,140 +147,105 @@ def tile_mix_mla_kernel(
         def c_quantize(cols):
             quantize(c_codes[:, cols], c_scales[:, cols], c_grouped[:, cols, :])
 
-        def c_store():
-            nc.sync.dma_start(out=out_2.rearrange("(p j) t -> p j t", j=PACK), in_=c_sb[:])
+        wk_grouped = sbuf("wk_grouped", [P, M, PACK], BF16)
+        wk_codes = sbuf("wk_codes", [P, M], I32)
+        wk_scales = sbuf("wk_scales", [P, M], U8)
+        kk_sb = [sbuf("kk_sb%d" % b, [P, T], F32) for b in range(4)]
+        wv_grouped = [sbuf("wv_grouped%d" % h, [P, HALF, PACK], BF16) for h in range(2)]
+        wv_codes = [sbuf("wv_codes%d" % h, [P, HALF], I32) for h in range(2)]
+        wv_scales = [sbuf("wv_scales%d" % h, [P, HALF], U8) for h in range(2)]
+        vv_sb = [sbuf("vv_sb%d" % h, [P, 2, T], F32) for h in range(2)]
 
-        def codes_store():
-            nc.sync.dma_start(out=out_3[0].rearrange("p t i -> p (t i)").bitcast(I32), in_=c_codes[:])
+        def wk_copy(engine, cols):
+            interleave(engine, wk_grouped[:, cols, :], wk_raw[:, :, cols])
 
-        def scales_store():
-            for quad in range(4):
-                nc.sync.dma_start(
-                    out=out_4[0, 4 * quad : 4 * quad + 4, :].bitcast(I32),
-                    in_=c_scales[32 * quad : 32 * quad + 4, :].bitcast(I32),
-                )
+        def wk_quantize(cols):
+            quantize(wk_codes[:, cols], wk_scales[:, cols], wk_grouped[:, cols, :])
 
-        up_raw = (wk_raw, wv_raw)
-        up_out = (out_0, out_1)
-        up_grouped = [[sbuf("up_grouped%d%d" % (u, h), [P, HALF, PACK], BF16) for h in range(2)] for u in range(2)]
-        up_codes = [[sbuf("up_codes%d%d" % (u, h), [P, HALF], I32) for h in range(2)] for u in range(2)]
-        up_scales = [[sbuf("up_scales%d%d" % (u, h), [P, HALF], U8) for h in range(2)] for u in range(2)]
-        up_sb = [[sbuf("up_sb%d%d" % (u, h), [P, 2, T], F32) for h in range(2)] for u in range(2)]
-
-        def up_bank(u, h, e):
-            return banks[4 * (1 - u) + 2 * h + e][:].rearrange("p j t -> p (j t)")
-
-        def up_copy(engine, u, h):
+        def wv_copy(engine, h):
             copy_on(
                 engine,
-                up_grouped[u][h][:].rearrange("p (e b m) j -> p b j m e", e=2, m=2),
-                up_raw[u][:, :, half(h)].rearrange("p j (b m e) -> p b j m e", e=2, m=2),
+                wv_grouped[h][:].rearrange("p (e b m) j -> p b j m e", e=2, m=2),
+                wv_raw[:, :, half(h)].rearrange("p j (b m e) -> p b j m e", e=2, m=2),
             )
 
-        def up_quantize(u, h):
-            quantize(up_codes[u][h][:], up_scales[u][h][:], up_grouped[u][h][:])
+        def wv_quantize(h):
+            quantize(wv_codes[h][:], wv_scales[h][:], wv_grouped[h][:])
 
-        def up_store_bank(u, h, e):
-            nc.sync.dma_start(
-                out=up_out[u][half(h), :].rearrange("(p e) t -> p e t", e=2)[:, e, :], in_=up_sb[u][h][:, e, :]
-            )
-
-        def upq(u, b, cols=slice(0, T)):
-            h, e = divmod(b, 2)
+        def up(bank, codes, scales, cols):
             nc.tensor.matmul_mx(
-                out=up_bank(u, h, e)[:, cols],
-                lhsT=up_codes[u][h][:, e * P : (e + 1) * P].bitcast(FP8X4),
-                lhsT_scale=up_scales[u][h][:, e * P : (e + 1) * P],
+                out=bank[:, cols],
+                lhsT=codes.bitcast(FP8X4),
+                lhsT_scale=scales,
                 rhs=c_codes[:, cols].bitcast(FP8X4),
                 rhs_scale=c_scales[:, cols],
                 start=True,
                 stop=True,
             )
 
-        def up(u, h):
+        def kk(b, cols=whole):
+            up(banks[4 + b], wk_codes[:, quarter(b)], wk_scales[:, quarter(b)], cols)
+
+        def vv(h):
             for e in range(2):
-                nc.tensor.matmul_mx(
-                    out=up_bank(u, h, e),
-                    lhsT=up_codes[u][h][:, e * P : (e + 1) * P].bitcast(FP8X4),
-                    lhsT_scale=up_scales[u][h][:, e * P : (e + 1) * P],
-                    rhs=c_codes[:].bitcast(FP8X4),
-                    rhs_scale=c_scales[:],
-                    start=True,
-                    stop=True,
-                )
+                up(banks[2 * h + e], wv_codes[h][:, e * P : (e + 1) * P], wv_scales[h][:, e * P : (e + 1) * P], whole)
 
-        def up_drain(engine, u, h, e):
-            copy_on(engine, up_sb[u][h][:, e, :], up_bank(u, h, e))
+        def kk_out(engine, b):
+            copy_on(engine, kk_sb[b][:], banks[4 + b][:])
+            nc.sync.dma_start(out=out_0[quarter(b), :], in_=kk_sb[b][:])
 
-        def up_store(u, h):
-            nc.sync.dma_start(
-                out=up_out[u][half(h), :].rearrange("(p e) t -> p e t", e=2), in_=up_sb[u][h][:]
-            )
+        def vv_out(h):
+            copy_on("scalar", vv_sb[h][:, 0, :], banks[2 * h][:])
+            copy_on("vector", vv_sb[h][:, 1, :], banks[2 * h + 1][:])
+            nc.sync.dma_start(out=out_1[half(h), :].rearrange("(p e) t -> p e t", e=2), in_=vv_sb[h][:])
 
-        for a in range(3):
-            x_copy("vector", a, quarter(0))
-            x_copy("scalar", a, quarter(2))
-            x_copy("vector", a, quarter(1))
-            x_copy("scalar", a, quarter(3))
-            for q in range(4):
-                x_quantize(a, quarter(q))
-                down(a, q)
         last = PASSES - 1
-        x_copy("vector", last, quarter(0))
-        x_copy("scalar", last, quarter(1))
-        x_copy("vector", last, slice(256, 320))
-        x_copy("scalar", last, quarter(3))
-        x_quantize(last, quarter(0))
-        w_deal(last, slice(0, 2))
-        w_deal(last, slice(2, 4))
-        down(last, 0)
-        x_quantize(last, quarter(1))
-        down(last, 1)
-        x_copy("vector", last, slice(320, 384))
-        x_quantize(last, quarter(3))
-        down(last, 3)
-        x_quantize(last, quarter(2))
-        down(last, 2)
-        c_drain("scalar", 0)
-        c_drain("vector", 1)
-        c_drain("scalar", 2)
-        c_drain("vector", 3)
-        c_store()
-        up_copy("vector", 0, 0)
-        c_round("vector", half(0))
-        c_round_psum("scalar", 2)
-        c_round_psum("scalar", 3)
-        up_copy("scalar", 0, 1)
-        up_quantize(0, 0)
+        for a in range(last):
+            x_copy("vector", a, half(0))
+            x_copy("scalar", a, half(1))
+            for h in range(2):
+                x_quantize(a, half(h))
+                down(a, h)
+        x_copy("vector", last, half(0))
+        x_copy("scalar", last, half(1))
+        w_deal(last)
+        for h in range(2):
+            x_quantize(last, half(h))
+            down(last, h)
+        for h in range(2):
+            c_drain("scalar", h, 0)
+            c_drain("vector", h, 1)
+        nc.sync.dma_start(out=out_2.rearrange("(p j) t -> p j t", j=PACK), in_=c_sb[:])
+        c_round("scalar", quarter(0))
+        c_round("vector", quarter(1))
+        wk_copy("scalar", quarter(0))
+        c_round("vector", half(1))
         c_quantize(half(0))
-        upq(0, 0, half(0))
+        wk_quantize(quarter(0))
+        kk(0, half(0))
         c_quantize(half(1))
-        upq(0, 0, half(1))
-        upq(0, 1)
-        codes_store()
-        scales_store()
-        up_copy("vector", 1, 0)
-        up_quantize(0, 1)
-        upq(0, 2)
-        upq(0, 3)
-        up_drain("scalar", 0, 0, 0)
-        up_store_bank(0, 0, 0)
-        up_drain("scalar", 0, 0, 1)
-        up_store_bank(0, 0, 1)
-        up_copy("vector", 1, 1)
-        up_quantize(1, 0)
-        upq(1, 0)
-        upq(1, 1)
-        up_quantize(1, 1)
-        upq(1, 2)
-        upq(1, 3)
-        up_drain("scalar", 0, 1, 0)
-        up_store_bank(0, 1, 0)
-        up_drain("vector", 0, 1, 1)
-        up_store_bank(0, 1, 1)
-        up_drain("scalar", 1, 0, 0)
-        up_drain("vector", 1, 0, 1)
-        up_store(1, 0)
-        up_drain("scalar", 1, 1, 0)
-        up_drain("vector", 1, 1, 1)
-        up_store(1, 1)
+        kk(0, half(1))
+        nc.sync.dma_start(out=out_3[0].rearrange("p t i -> p (t i)").bitcast(I32), in_=c_codes[:])
+        for quad in range(4):
+            nc.sync.dma_start(
+                out=out_4[0, 4 * quad : 4 * quad + 4, :].bitcast(I32),
+                in_=c_scales[32 * quad : 32 * quad + 4, :].bitcast(I32),
+            )
+        wk_copy("scalar", quarter(1))
+        wk_copy("scalar", quarter(2))
+        wk_copy("vector", quarter(3))
+        wk_quantize(quarter(1))
+        kk(1)
+        wv_copy("vector", 0)
+        wk_quantize(half(1))
+        kk(2)
+        kk(3)
+        for b in range(4):
+            kk_out("scalar", b)
+        wv_quantize(0)
+        vv(0)
+        wv_copy("vector", 1)
+        wv_quantize(1)
+        vv(1)
+        for h in range(2):
+            vv_out(h)

@@ -90,10 +90,10 @@ def tile_mix_mla_kernel(
         w_codes = [sbuf("w_codes%d" % a, [P, R], I32) for a in range(PASSES)]
         w_scales = sbuf("w_scales", [P, R], U8)
 
-        def w_deal(a):
+        def w_deal(a, slots=slice(0, PACK)):
             nc.vector.tensor_copy(
-                out=w_codes[a][:].rearrange("p (j b m) -> p b j m", j=PACK, m=4),
-                in_=w_raw[a].rearrange("p (b m j) -> p b j m", j=PACK, m=4),
+                out=w_codes[a][:].rearrange("p (j b m) -> p b j m", j=PACK, m=4)[:, :, slots, :],
+                in_=w_raw[a].rearrange("p (b m j) -> p b j m", j=PACK, m=4)[:, :, slots, :],
             )
 
         for a in range(PASSES - 1):
@@ -113,20 +113,20 @@ def tile_mix_mla_kernel(
         def x_quantize(a, cols):
             quantize(x_codes[a][:, cols], x_scales[a][:, cols], x_grouped[a][:, cols, :])
 
-        def c_bank(h, pair):
-            return banks[2 * h + pair]
+        def c_bank(h, j):
+            return banks[PACK * h + j][:, half(0)]
 
-        def down(a, h):
+        def down(a, h, slots=range(PACK)):
             cols = half(h)
-            for j in range(PACK):
+            for j in slots:
                 nc.tensor.matmul_mx(
-                    out=c_bank(h, j // 2)[:, half(j % 2)],
+                    out=c_bank(h, j),
                     lhsT=w_codes[a][:, j * P : (j + 1) * P].bitcast(FP8X4),
                     lhsT_scale=w_scales[4 * a : P, j * P : (j + 1) * P],
                     rhs=x_codes[a][:, cols].bitcast(FP8X4),
                     rhs_scale=x_scales[a][:, cols],
-                    start=(a == 0 and j % 2 == 0),
-                    stop=(a == PASSES - 1 and j % 2 == 1),
+                    start=(a == 0),
+                    stop=(a == PASSES - 1),
                 )
 
         c_sb = sbuf("c_sb", [P, PACK, T], F32)
@@ -134,12 +134,11 @@ def tile_mix_mla_kernel(
         c_codes = sbuf("c_codes", [P, T], I32)
         c_scales = sbuf("c_scales", [P, T], U8)
 
-        def c_drain(engine, h, pair):
-            copy_on(
-                engine,
-                c_sb[:, 2 * pair : 2 * pair + 2, half(h)],
-                c_bank(h, pair)[:].rearrange("p (j t) -> p j t", j=2),
-            )
+        def c_drain(engine, h, j):
+            copy_on(engine, c_sb[:, j, half(h)], c_bank(h, j))
+
+        def c_store(slots):
+            nc.sync.dma_start(out=out_2.rearrange("(p j) t -> p j t", j=PACK)[:, slots, :], in_=c_sb[:, slots, :])
 
         def c_round(engine, cols):
             interleave(engine, c_grouped[:, cols, :], c_sb[:, :, cols])
@@ -183,15 +182,19 @@ def tile_mix_mla_kernel(
                 stop=True,
             )
 
-        def kk(b, cols=whole):
-            up(banks[4 + b], wk_codes[:, quarter(b)], wk_scales[:, quarter(b)], cols)
+        def kk(b, cols=whole, bank=None):
+            bank = banks[4 + b] if bank is None else bank
+            up(bank, wk_codes[:, quarter(b)], wk_scales[:, quarter(b)], cols)
 
         def vv(h):
             for e in range(2):
                 up(banks[2 * h + e], wv_codes[h][:, e * P : (e + 1) * P], wv_scales[h][:, e * P : (e + 1) * P], whole)
 
-        def kk_out(engine, b):
-            copy_on(engine, kk_sb[b][:], banks[4 + b][:])
+        def kk_drain(engine, b, cols=whole, bank=None):
+            bank = banks[4 + b] if bank is None else bank
+            copy_on(engine, kk_sb[b][:, cols], bank[:, cols])
+
+        def kk_store(b):
             nc.sync.dma_start(out=out_0[quarter(b), :], in_=kk_sb[b][:])
 
         def vv_out(h):
@@ -206,25 +209,29 @@ def tile_mix_mla_kernel(
             for h in range(2):
                 x_quantize(a, half(h))
                 down(a, h)
-        x_copy("vector", last, half(0))
-        x_copy("scalar", last, half(1))
-        w_deal(last)
+        x_copy("vector", last, slice(0, 288))
+        x_copy("scalar", last, slice(288, T))
+        w_deal(last, slice(0, 2))
+        x_quantize(last, half(0))
+        w_deal(last, slice(2, 4))
+        down(last, 0)
+        x_quantize(last, half(1))
+        down(last, 1)
         for h in range(2):
-            x_quantize(last, half(h))
-            down(last, h)
-        for h in range(2):
-            c_drain("scalar", h, 0)
-            c_drain("vector", h, 1)
-        nc.sync.dma_start(out=out_2.rearrange("(p j) t -> p j t", j=PACK), in_=c_sb[:])
-        c_round("scalar", quarter(0))
-        c_round("vector", quarter(1))
+            for j in range(PACK):
+                c_drain("scalar" if j % 2 == 0 else "vector", h, j)
+        c_store(slice(0, PACK))
         wk_copy("scalar", quarter(0))
-        c_round("vector", half(1))
-        c_quantize(half(0))
+        c_round("vector", half(0))
+        c_round("scalar", quarter(3))
+        c_round("vector", quarter(2))
         wk_quantize(quarter(0))
+        c_quantize(half(0))
         kk(0, half(0))
-        c_quantize(half(1))
-        kk(0, half(1))
+        c_quantize(quarter(2))
+        kk(0, quarter(2))
+        c_quantize(quarter(3))
+        kk(0, quarter(3), banks[0])
         nc.sync.dma_start(out=out_3[0].rearrange("p t i -> p (t i)").bitcast(I32), in_=c_codes[:])
         for quad in range(4):
             nc.sync.dma_start(
@@ -232,16 +239,25 @@ def tile_mix_mla_kernel(
                 in_=c_scales[32 * quad : 32 * quad + 4, :].bitcast(I32),
             )
         wk_copy("scalar", quarter(1))
-        wk_copy("scalar", quarter(2))
         wk_copy("vector", quarter(3))
         wk_quantize(quarter(1))
-        kk(1)
-        wv_copy("vector", 0)
-        wk_quantize(half(1))
-        kk(2)
+        kk(1, half(0))
+        kk(1, half(1), banks[1])
+        wk_quantize(quarter(3))
         kk(3)
-        for b in range(4):
-            kk_out("scalar", b)
+        wk_copy("scalar", quarter(2))
+        kk_drain("scalar", 0, slice(0, 3 * QUARTER))
+        kk_drain("scalar", 0, quarter(3), banks[0])
+        kk_store(0)
+        wv_copy("vector", 0)
+        wk_quantize(quarter(2))
+        kk(2)
+        kk_drain("scalar", 1, half(0))
+        kk_drain("scalar", 1, half(1), banks[1])
+        kk_store(1)
+        for b in (3, 2):
+            kk_drain("scalar", b)
+            kk_store(b)
         wv_quantize(0)
         vv(0)
         wv_copy("vector", 1)

@@ -1,3 +1,4 @@
+import math
 from contextlib import ExitStack
 
 import concourse.mybir as mybir
@@ -18,6 +19,10 @@ PASSES = K // K_PASS
 QUARTER = T // 4
 HALF = T // 2
 ALIGN = 256
+LOAD_SHIFT = 0
+STORE_SHIFT = 192
+OTHER_SHIFT = 0
+BYTES_OF = {F32: 4, I32: 4, BF16: 2, U8: 1}
 
 
 def tile_mix_mla_kernel(
@@ -29,8 +34,12 @@ def tile_mix_mla_kernel(
         ps = ctx.enter_context(tc.psum_pool(name="ps", bufs=1))
         ctx.enter_context(tc.manual_schedule())
 
-        def sbuf(name, shape, dtype):
-            return sb.tile(shape, dtype, name=name, align_bytes=ALIGN)
+        used = [0]
+
+        def sbuf(name, shape, dtype, shift=OTHER_SHIFT):
+            start = used[0] + shift
+            used[0] = start + math.prod(shape[1:]) * BYTES_OF[dtype] + (ALIGN - shift) % ALIGN
+            return sb.tile(shape, dtype, name=name, offset=start, align_bytes=math.gcd(ALIGN, shift))
 
         def copy_on(engine, out, in_):
             if engine == "vector":
@@ -62,14 +71,14 @@ def tile_mix_mla_kernel(
 
         banks = [ps.tile([P, T], F32, name="bank%d" % b) for b in range(8)]
 
-        w_early = sbuf("w_early", [P, PASSES - 1, R], I32)
-        w_last = sbuf("w_last", [P, R], I32)
+        w_early = sbuf("w_early", [P, PASSES - 1, R], I32, LOAD_SHIFT)
+        w_last = sbuf("w_last", [P, R], I32, LOAD_SHIFT)
         w_raw = [w_early[:, a, :] for a in range(PASSES - 1)] + [w_last[:]]
         w_words = w8_words.rearrange("a p r i -> p a (r i)").bitcast(I32)
-        ws_raw = sbuf("ws_raw", [P, R], U8)
-        x_raw = [sbuf("x_raw%d" % a, [P, PACK, T], F32) for a in range(PASSES)]
-        wk_raw = sbuf("wk_raw", [P, PACK, M], F32)
-        wv_raw = sbuf("wv_raw", [P, PACK, N], F32)
+        ws_raw = sbuf("ws_raw", [P, R], U8, LOAD_SHIFT)
+        x_raw = [sbuf("x_raw%d" % a, [P, PACK, T], F32, LOAD_SHIFT) for a in range(PASSES)]
+        wk_raw = sbuf("wk_raw", [P, PACK, M], F32, LOAD_SHIFT)
+        wv_raw = sbuf("wv_raw", [P, PACK, N], F32, LOAD_SHIFT)
 
         nc.vector.memset(ws_raw[:].bitcast(I32), 0)
         nc.sync.dma_start(out=w_early[:], in_=w_words[:, 0 : PASSES - 1, :])
@@ -129,10 +138,10 @@ def tile_mix_mla_kernel(
                     stop=(a == PASSES - 1),
                 )
 
-        c_sb = sbuf("c_sb", [P, PACK, T], F32)
+        c_sb = sbuf("c_sb", [P, PACK, T], F32, STORE_SHIFT)
         c_grouped = sbuf("c_grouped", [P, T, PACK], BF16)
-        c_codes = sbuf("c_codes", [P, T], I32)
-        c_scales = sbuf("c_scales", [P, T], U8)
+        c_codes = sbuf("c_codes", [P, T], I32, STORE_SHIFT)
+        c_scales = sbuf("c_scales", [P, T], U8, STORE_SHIFT)
 
         def c_drain(engine, h, j):
             copy_on(engine, c_sb[:, j, half(h)], c_bank(h, j))
@@ -149,11 +158,11 @@ def tile_mix_mla_kernel(
         wk_grouped = sbuf("wk_grouped", [P, M, PACK], BF16)
         wk_codes = sbuf("wk_codes", [P, M], I32)
         wk_scales = sbuf("wk_scales", [P, M], U8)
-        kk_sb = [sbuf("kk_sb%d" % b, [P, T], F32) for b in range(4)]
+        kk_sb = [sbuf("kk_sb%d" % b, [P, T], F32, STORE_SHIFT) for b in range(4)]
         wv_grouped = [sbuf("wv_grouped%d" % h, [P, HALF, PACK], BF16) for h in range(2)]
         wv_codes = [sbuf("wv_codes%d" % h, [P, HALF], I32) for h in range(2)]
         wv_scales = [sbuf("wv_scales%d" % h, [P, HALF], U8) for h in range(2)]
-        vv_sb = [sbuf("vv_sb%d" % h, [P, 2, T], F32) for h in range(2)]
+        vv_sb = [sbuf("vv_sb%d" % h, [P, 2, T], F32, STORE_SHIFT) for h in range(2)]
 
         def wk_copy(engine, cols):
             interleave(engine, wk_grouped[:, cols, :], wk_raw[:, :, cols])

@@ -80,13 +80,22 @@ def tile_mix_mla_kernel(
         wk_raw = sbuf("wk_raw", [P, PACK, M], F32, LOAD_SHIFT)
         wv_raw = sbuf("wv_raw", [P, PACK, N], F32, LOAD_SHIFT)
 
+        ws_upper = sbuf("ws_upper", [P, R], U8, LOAD_SHIFT)
+
+        def scale_rows(tile, quad):
+            return tile[32 * quad : 32 * quad + 16, :].bitcast(I32)
+
+        def scale_load(queue, tile, quad):
+            queue.dma_start(out=scale_rows(tile, quad), in_=w8_scales[:, 4 * quad : 4 * quad + 4, :].bitcast(I32))
+
         nc.vector.memset(ws_raw[:].bitcast(I32), 0)
+        scale_load(nc.scalar, ws_upper, 2)
+        scale_load(nc.sync, ws_upper, 3)
         nc.sync.dma_start(out=w_early[:], in_=w_words[:, 0 : PASSES - 1, :])
-        for quad in range(4):
-            nc.sync.dma_start(
-                out=ws_raw[32 * quad : 32 * quad + 16, :].bitcast(I32),
-                in_=w8_scales[:, 4 * quad : 4 * quad + 4, :].bitcast(I32),
-            )
+        scale_load(nc.sync, ws_raw, 0)
+        scale_load(nc.sync, ws_raw, 1)
+        for quad in (2, 3):
+            nc.vector.tensor_copy(out=scale_rows(ws_raw, quad), in_=scale_rows(ws_upper, quad))
         for a in range(PASSES):
             nc.sync.dma_start(
                 out=x_raw[a][:],

@@ -1,4 +1,3 @@
-import math
 from contextlib import ExitStack
 
 import concourse.mybir as mybir
@@ -19,10 +18,6 @@ PASSES = K // K_PASS
 QUARTER = T // 4
 HALF = T // 2
 ALIGN = 256
-LOAD_SHIFT = 0
-STORE_SHIFT = 192
-OTHER_SHIFT = 0
-BYTES_OF = {F32: 4, I32: 4, BF16: 2, U8: 1}
 
 
 def tile_mix_mla_kernel(
@@ -34,12 +29,8 @@ def tile_mix_mla_kernel(
         ps = ctx.enter_context(tc.psum_pool(name="ps", bufs=1))
         ctx.enter_context(tc.manual_schedule())
 
-        used = [0]
-
-        def sbuf(name, shape, dtype, shift=OTHER_SHIFT):
-            start = used[0] + shift
-            used[0] = start + math.prod(shape[1:]) * BYTES_OF[dtype] + (ALIGN - shift) % ALIGN
-            return sb.tile(shape, dtype, name=name, offset=start, align_bytes=math.gcd(ALIGN, shift))
+        def sbuf(name, shape, dtype):
+            return sb.tile(shape, dtype, name=name, align_bytes=ALIGN)
 
         def copy_on(engine, out, in_):
             if engine == "vector":
@@ -71,29 +62,29 @@ def tile_mix_mla_kernel(
 
         banks = [ps.tile([P, T], F32, name="bank%d" % b) for b in range(8)]
 
-        w_early = sbuf("w_early", [P, PASSES - 1, R], I32, LOAD_SHIFT)
-        w_last = sbuf("w_last", [P, R], I32, LOAD_SHIFT)
+        w_early = sbuf("w_early", [P, PASSES - 1, R], I32)
+        w_last = sbuf("w_last", [P, R], I32)
         w_raw = [w_early[:, a, :] for a in range(PASSES - 1)] + [w_last[:]]
         w_words = w8_words.rearrange("a p r i -> p a (r i)").bitcast(I32)
-        ws_raw = sbuf("ws_raw", [P, R], U8, LOAD_SHIFT)
-        x_raw = [sbuf("x_raw%d" % a, [P, PACK, T], F32, LOAD_SHIFT) for a in range(PASSES)]
-        wk_raw = sbuf("wk_raw", [P, PACK, M], F32, LOAD_SHIFT)
-        wv_raw = sbuf("wv_raw", [P, PACK, N], F32, LOAD_SHIFT)
+        ws_raw = sbuf("ws_raw", [P, R], U8)
+        x_raw = [sbuf("x_raw%d" % a, [P, PACK, T], F32) for a in range(PASSES)]
+        wk_raw = sbuf("wk_raw", [P, PACK, M], F32)
+        wv_raw = sbuf("wv_raw", [P, PACK, N], F32)
 
-        ws_upper = sbuf("ws_upper", [P, R], U8, LOAD_SHIFT)
+        ws_upper = sbuf("ws_upper", [P, R], U8)
 
         def scale_rows(tile, quad):
             return tile[32 * quad : 32 * quad + 16, :].bitcast(I32)
 
-        def scale_load(queue, tile, quad):
-            queue.dma_start(out=scale_rows(tile, quad), in_=w8_scales[:, 4 * quad : 4 * quad + 4, :].bitcast(I32))
+        def scale_load(tile, quad):
+            nc.sync.dma_start(out=scale_rows(tile, quad), in_=w8_scales[:, 4 * quad : 4 * quad + 4, :].bitcast(I32))
 
         nc.vector.memset(ws_raw[:].bitcast(I32), 0)
-        scale_load(nc.scalar, ws_upper, 2)
-        scale_load(nc.sync, ws_upper, 3)
+        for quad in (2, 3):
+            scale_load(ws_upper, quad)
         nc.sync.dma_start(out=w_early[:], in_=w_words[:, 0 : PASSES - 1, :])
-        scale_load(nc.sync, ws_raw, 0)
-        scale_load(nc.sync, ws_raw, 1)
+        for quad in (0, 1):
+            scale_load(ws_raw, quad)
         for quad in (2, 3):
             nc.vector.tensor_copy(out=scale_rows(ws_raw, quad), in_=scale_rows(ws_upper, quad))
         for a in range(PASSES):
@@ -147,10 +138,10 @@ def tile_mix_mla_kernel(
                     stop=(a == PASSES - 1),
                 )
 
-        c_sb = sbuf("c_sb", [P, PACK, T], F32, STORE_SHIFT)
+        c_sb = sbuf("c_sb", [P, PACK, T], F32)
         c_grouped = sbuf("c_grouped", [P, T, PACK], BF16)
-        c_codes = sbuf("c_codes", [P, T], I32, STORE_SHIFT)
-        c_scales = sbuf("c_scales", [P, T], U8, STORE_SHIFT)
+        c_codes = sbuf("c_codes", [P, T], I32)
+        c_scales = sbuf("c_scales", [P, T], U8)
 
         def c_drain(engine, h, j):
             copy_on(engine, c_sb[:, j, half(h)], c_bank(h, j))
@@ -167,11 +158,11 @@ def tile_mix_mla_kernel(
         wk_grouped = sbuf("wk_grouped", [P, M, PACK], BF16)
         wk_codes = sbuf("wk_codes", [P, M], I32)
         wk_scales = sbuf("wk_scales", [P, M], U8)
-        kk_sb = [sbuf("kk_sb%d" % b, [P, T], F32, STORE_SHIFT) for b in range(4)]
+        kk_sb = [sbuf("kk_sb%d" % b, [P, T], F32) for b in range(4)]
         wv_grouped = [sbuf("wv_grouped%d" % h, [P, HALF, PACK], BF16) for h in range(2)]
         wv_codes = [sbuf("wv_codes%d" % h, [P, HALF], I32) for h in range(2)]
         wv_scales = [sbuf("wv_scales%d" % h, [P, HALF], U8) for h in range(2)]
-        vv_sb = [sbuf("vv_sb%d" % h, [P, 2, T], F32, STORE_SHIFT) for h in range(2)]
+        vv_sb = [sbuf("vv_sb%d" % h, [P, 2, T], F32) for h in range(2)]
 
         def wk_copy(engine, cols):
             interleave(engine, wk_grouped[:, cols, :], wk_raw[:, :, cols])
@@ -251,11 +242,6 @@ def tile_mix_mla_kernel(
         c_quantize(quarter(3))
         kk(0, quarter(3), banks[0])
         nc.sync.dma_start(out=out_3[0].rearrange("p t i -> p (t i)").bitcast(I32), in_=c_codes[:])
-        for quad in range(4):
-            nc.sync.dma_start(
-                out=out_4[0, 4 * quad : 4 * quad + 4, :].bitcast(I32),
-                in_=c_scales[32 * quad : 32 * quad + 4, :].bitcast(I32),
-            )
         wk_copy("scalar", quarter(1))
         wk_copy("vector", quarter(3))
         wk_quantize(quarter(1))
@@ -283,3 +269,8 @@ def tile_mix_mla_kernel(
         vv(1)
         for h in range(2):
             vv_out(h)
+        for quad in range(4):
+            nc.sync.dma_start(
+                out=out_4[0, 4 * quad : 4 * quad + 4, :].bitcast(I32),
+                in_=c_scales[32 * quad : 32 * quad + 4, :].bitcast(I32),
+            )

@@ -199,6 +199,17 @@ def tile_mix_mla_kernel(
             for e in range(2):
                 up(banks[2 * h + e], wv_codes[h][:, e * P : (e + 1) * P], wv_scales[h][:, e * P : (e + 1) * P], whole)
 
+        def warm_up(codes, scales):
+            nc.tensor.matmul_mx(
+                out=banks[7][:],
+                lhsT=codes.bitcast(FP8X4),
+                lhsT_scale=scales,
+                rhs=x_codes[PASSES - 1][:].bitcast(FP8X4),
+                rhs_scale=x_scales[PASSES - 1][:],
+                start=True,
+                stop=True,
+            )
+
         def kk_drain(engine, b, cols=whole, bank=None):
             bank = banks[4 + b] if bank is None else bank
             copy_on(engine, kk_sb[b][:, cols], bank[:, cols])
@@ -230,11 +241,14 @@ def tile_mix_mla_kernel(
             for j in range(PACK):
                 c_drain("scalar" if j % 2 == 0 else "vector", h, j)
         c_store(slice(0, PACK))
+        for n in range(2):
+            warm_up(w_codes[last][:, quarter(n)], w_scales[4 * last : P, quarter(n)])
         wk_copy("scalar", quarter(0))
         c_round("vector", half(0))
         c_round("scalar", quarter(3))
         c_round("vector", quarter(2))
         wk_quantize(quarter(0))
+        warm_up(wk_codes[:, quarter(0)], wk_scales[:, quarter(0)])
         c_quantize(half(0))
         kk(0, half(0))
         c_quantize(quarter(2))

@@ -155,6 +155,12 @@ def tile_mix_mla_kernel(
         def c_quantize(cols):
             quantize(c_codes[:, cols], c_scales[:, cols], c_grouped[:, cols, :])
 
+        def scales_store(quad):
+            nc.sync.dma_start(
+                out=out_4[0, 4 * quad : 4 * quad + 4, :].bitcast(I32),
+                in_=c_scales[32 * quad : 32 * quad + 4, :].bitcast(I32),
+            )
+
         wk_grouped = sbuf("wk_grouped", [P, M, PACK], BF16)
         wk_codes = sbuf("wk_codes", [P, M], I32)
         wk_scales = sbuf("wk_scales", [P, M], U8)
@@ -256,6 +262,8 @@ def tile_mix_mla_kernel(
         c_quantize(quarter(3))
         kk(0, quarter(3), banks[0])
         nc.sync.dma_start(out=out_3[0].rearrange("p t i -> p (t i)").bitcast(I32), in_=c_codes[:])
+        for quad in (2, 3):
+            scales_store(quad)
         wk_copy("scalar", quarter(1))
         wk_copy("vector", quarter(3))
         wk_quantize(quarter(1))
@@ -283,8 +291,5 @@ def tile_mix_mla_kernel(
         vv(1)
         for h in range(2):
             vv_out(h)
-        for quad in range(4):
-            nc.sync.dma_start(
-                out=out_4[0, 4 * quad : 4 * quad + 4, :].bitcast(I32),
-                in_=c_scales[32 * quad : 32 * quad + 4, :].bitcast(I32),
-            )
+        for quad in (0, 1):
+            scales_store(quad)

@@ -262,7 +262,7 @@ def tile_mix_mla_kernel(
         c_quantize(quarter(3))
         kk(0, quarter(3), banks[0])
         nc.sync.dma_start(out=out_3[0].rearrange("p t i -> p (t i)").bitcast(I32), in_=c_codes[:])
-        for quad in (2, 3):
+        for quad in (2, 3, 0, 1):
             scales_store(quad)
         wk_copy("scalar", quarter(1))
         wk_copy("vector", quarter(3))
@@ -291,5 +291,3 @@ def tile_mix_mla_kernel(
         vv(1)
         for h in range(2):
             vv_out(h)
-        for quad in (0, 1):
-            scales_store(quad)

@@ -155,10 +155,10 @@ def tile_mix_mla_kernel(
         def c_quantize(cols):
             quantize(c_codes[:, cols], c_scales[:, cols], c_grouped[:, cols, :])
 
-        def scales_store(quad):
+        def scales_store(row):
             nc.sync.dma_start(
-                out=out_4[0, 4 * quad : 4 * quad + 4, :].bitcast(I32),
-                in_=c_scales[32 * quad : 32 * quad + 4, :].bitcast(I32),
+                out=out_4[0, row : 16 : 4, :].bitcast(I32),
+                in_=c_scales[row : P : 32, :].bitcast(I32),
             )
 
         wk_grouped = sbuf("wk_grouped", [P, M, PACK], BF16)
@@ -235,8 +235,8 @@ def tile_mix_mla_kernel(
             for h in range(2):
                 x_quantize(a, half(h))
                 down(a, h)
-        x_copy("vector", last, slice(0, 288))
-        x_copy("scalar", last, slice(288, T))
+        x_copy("vector", last, half(0))
+        x_copy("scalar", last, half(1))
         w_deal(last, slice(0, 2))
         x_quantize(last, half(0))
         w_deal(last, slice(2, 4))
@@ -257,13 +257,11 @@ def tile_mix_mla_kernel(
         warm_up(wk_codes[:, quarter(0)], wk_scales[:, quarter(0)])
         c_quantize(half(0))
         kk(0, half(0))
-        c_quantize(quarter(2))
-        kk(0, quarter(2))
-        c_quantize(quarter(3))
-        kk(0, quarter(3), banks[0])
+        c_quantize(half(1))
+        kk(0, half(1), banks[0])
         nc.sync.dma_start(out=out_3[0].rearrange("p t i -> p (t i)").bitcast(I32), in_=c_codes[:])
-        for quad in (2, 3, 0, 1):
-            scales_store(quad)
+        for row in range(4):
+            scales_store(row)
         wk_copy("scalar", quarter(1))
         wk_copy("vector", quarter(3))
         wk_quantize(quarter(1))
@@ -272,8 +270,8 @@ def tile_mix_mla_kernel(
         wk_quantize(quarter(3))
         kk(3)
         wk_copy("scalar", quarter(2))
-        kk_drain("scalar", 0, slice(0, 3 * QUARTER))
-        kk_drain("scalar", 0, quarter(3), banks[0])
+        kk_drain("scalar", 0, half(0))
+        kk_drain("scalar", 0, half(1), banks[0])
         kk_store(0)
         wv_copy("vector", 0)
         wk_quantize(quarter(2))

@@ -201,9 +201,11 @@ def tile_mix_mla_kernel(
             bank = banks[4 + b] if bank is None else bank
             up(bank, wk_codes[:, quarter(b)], wk_scales[:, quarter(b)], cols)
 
+        vv_banks = [banks[3], banks[1], banks[4], banks[5]]
+
         def vv(h):
             for e in range(2):
-                up(banks[2 * h + e], wv_codes[h][:, e * P : (e + 1) * P], wv_scales[h][:, e * P : (e + 1) * P], whole)
+                up(vv_banks[2 * h + e], wv_codes[h][:, e * P : (e + 1) * P], wv_scales[h][:, e * P : (e + 1) * P], whole)
 
         def warm_up(codes, scales):
             nc.tensor.matmul_mx(
@@ -224,8 +226,8 @@ def tile_mix_mla_kernel(
             nc.sync.dma_start(out=out_0[quarter(b), :], in_=kk_sb[b][:])
 
         def vv_out(h):
-            copy_on("scalar", vv_sb[h][:, 0, :], banks[2 * h][:])
-            copy_on("vector", vv_sb[h][:, 1, :], banks[2 * h + 1][:])
+            copy_on("scalar", vv_sb[h][:, 0, :], vv_banks[2 * h][:])
+            copy_on("vector", vv_sb[h][:, 1, :], vv_banks[2 * h + 1][:])
             nc.sync.dma_start(out=out_1[half(h), :].rearrange("(p e) t -> p e t", e=2), in_=vv_sb[h][:])
 
         last = PASSES - 1
@@ -235,8 +237,10 @@ def tile_mix_mla_kernel(
             for h in range(2):
                 x_quantize(a, half(h))
                 down(a, h)
-        x_copy("vector", last, half(0))
-        x_copy("scalar", last, half(1))
+        x_copy("vector", last, slice(0, 176))
+        x_copy("scalar", last, slice(176, HALF))
+        x_copy("vector", last, slice(400, T))
+        x_copy("scalar", last, slice(HALF, 400))
         w_deal(last, slice(0, 2))
         x_quantize(last, half(0))
         w_deal(last, slice(2, 4))
@@ -250,41 +254,37 @@ def tile_mix_mla_kernel(
         for n in range(2):
             warm_up(w_codes[last][:, quarter(n)], w_scales[4 * last : P, quarter(n)])
         wk_copy("scalar", quarter(0))
-        c_round("vector", half(0))
-        c_round("scalar", quarter(3))
-        c_round("vector", quarter(2))
-        wk_quantize(quarter(0))
+        wk_copy("vector", quarter(1))
+        c_round("scalar", slice(352, T))
+        c_round("vector", slice(0, 352))
+        wk_quantize(half(0))
         warm_up(wk_codes[:, quarter(0)], wk_scales[:, quarter(0)])
         c_quantize(half(0))
         kk(0, half(0))
+        kk(1, half(0))
         c_quantize(half(1))
         kk(0, half(1), banks[0])
+        kk(1, half(1), banks[1])
         nc.sync.dma_start(out=out_3[0].rearrange("p t i -> p (t i)").bitcast(I32), in_=c_codes[:])
         for row in range(4):
             scales_store(row)
-        wk_copy("scalar", quarter(1))
-        wk_copy("vector", quarter(3))
-        wk_quantize(quarter(1))
-        kk(1, half(0))
-        kk(1, half(1), banks[1])
-        wk_quantize(quarter(3))
-        kk(3)
         wk_copy("scalar", quarter(2))
-        kk_drain("scalar", 0, half(0))
-        kk_drain("scalar", 0, half(1), banks[0])
-        kk_store(0)
-        wv_copy("vector", 0)
+        wk_copy("scalar", quarter(3))
         wk_quantize(quarter(2))
         kk(2)
-        kk_drain("scalar", 1, half(0))
-        kk_drain("scalar", 1, half(1), banks[1])
-        kk_store(1)
-        for b in (3, 2):
-            kk_drain("scalar", b)
+        wv_copy("vector", 0)
+        wk_quantize(quarter(3))
+        kk(3)
+        for b in range(2):
+            kk_drain("scalar", b, half(0))
+            kk_drain("scalar", b, half(1), banks[b])
             kk_store(b)
         wv_quantize(0)
         vv(0)
         wv_copy("vector", 1)
+        for b in (2, 3):
+            kk_drain("scalar", b)
+            kk_store(b)
         wv_quantize(1)
         vv(1)
         for h in range(2):

@@ -258,7 +258,6 @@ def tile_mix_mla_kernel(
         c_round("scalar", slice(352, T))
         c_round("vector", slice(0, 352))
         wk_quantize(half(0))
-        warm_up(wk_codes[:, quarter(0)], wk_scales[:, quarter(0)])
         c_quantize(half(0))
         kk(0, half(0))
         kk(1, half(0))

from contextlib import ExitStack

import concourse.mybir as mybir

K, R, M, N, T = 2048, 512, 512, 512, 512
FLOPS = 2 * K * R * T + 2 * R * M * T + 2 * R * N * T

F32 = mybir.dt.float32
BF16 = mybir.dt.bfloat16
I32 = mybir.dt.int32
U8 = mybir.dt.uint8
FP8X4 = mybir.dt.float8_e4m3fn_x4

P = 128
PACK = 4
K_PASS = P * PACK
PASSES = K // K_PASS
QUARTER = T // 4
HALF = T // 2
ALIGN = 256


def tile_mix_mla_kernel(
    tc, x, w8_words, w8_scales, wk, wv, out_0, out_1, out_2, out_3, out_4
):
    nc = tc.nc
    with ExitStack() as ctx:
        sb = ctx.enter_context(tc.tile_pool(name="sb", bufs=1))
        ps = ctx.enter_context(tc.psum_pool(name="ps", bufs=1))
        ctx.enter_context(tc.manual_schedule())

        def sbuf(name, shape, dtype):
            return sb.tile(shape, dtype, name=name, align_bytes=ALIGN)

        def copy_on(engine, out, in_):
            if engine == "vector":
                nc.vector.tensor_copy(out=out, in_=in_)
            else:
                nc.scalar.copy(out=out, in_=in_)

        def interleave(engine, grouped, rows):
            copy_on(
                engine,
                grouped.rearrange("p (c i) j -> p c j i", i=4),
                rows.rearrange("p j (c i) -> p c j i", i=4),
            )

        def quantize(codes, scales, grouped):
            nc.vector.quantize_mx(
                out=codes.bitcast(FP8X4),
                scales=scales,
                in_=grouped.rearrange("p c j -> p (c j)"),
            )

        def quarter(q):
            return slice(q * QUARTER, (q + 1) * QUARTER)

        def half(h):
            return slice(h * HALF, (h + 1) * HALF)

        whole = slice(0, T)

        banks = [ps.tile([P, T], F32, name="bank%d" % b) for b in range(8)]

        w_early = sbuf("w_early", [P, PASSES - 1, R], I32)
        w_last = sbuf("w_last", [P, R], I32)
        w_raw = [w_early[:, a, :] for a in range(PASSES - 1)] + [w_last[:]]
        w_words = w8_words.rearrange("a p r i -> p a (r i)").bitcast(I32)
        ws_raw = sbuf("ws_raw", [P, R], U8)
        x_raw = [sbuf("x_raw%d" % a, [P, PACK, T], F32) for a in range(PASSES)]
        wk_raw = sbuf("wk_raw", [P, PACK, M], F32)
        wv_raw = sbuf("wv_raw", [P, PACK, N], F32)

        ws_upper = sbuf("ws_upper", [P, R], U8)

        def scale_rows(tile, quad):
            return tile[32 * quad : 32 * quad + 16, :].bitcast(I32)

        def scale_load(tile, quad):
            nc.sync.dma_start(out=scale_rows(tile, quad), in_=w8_scales[:, 4 * quad : 4 * quad + 4, :].bitcast(I32))

        nc.vector.memset(ws_raw[:].bitcast(I32), 0)
        for quad in (2, 3):
            scale_load(ws_upper, quad)
        nc.sync.dma_start(out=w_early[:], in_=w_words[:, 0 : PASSES - 1, :])
        for quad in (0, 1):
            scale_load(ws_raw, quad)
        for quad in (2, 3):
            nc.vector.tensor_copy(out=scale_rows(ws_raw, quad), in_=scale_rows(ws_upper, quad))
        for a in range(PASSES):
            nc.sync.dma_start(
                out=x_raw[a][:],
                in_=x[a * K_PASS : (a + 1) * K_PASS, :].rearrange("(p j) t -> p j t", j=PACK),
            )
        nc.sync.dma_start(out=w_last[:], in_=w_words[:, PASSES - 1, :])
        nc.sync.dma_start(out=wk_raw[:], in_=wk.rearrange("(p j) m -> p j m", j=PACK))
        nc.sync.dma_start(out=wv_raw[:], in_=wv.rearrange("(p j) n -> p j n", j=PACK))

        w_codes = [sbuf("w_codes%d" % a, [P, R], I32) for a in range(PASSES)]
        w_scales = sbuf("w_scales", [P, R], U8)

        def w_deal(a, slots=slice(0, PACK)):
            nc.vector.tensor_copy(
                out=w_codes[a][:].rearrange("p (j b m) -> p b j m", j=PACK, m=4)[:, :, slots, :],
                in_=w_raw[a].rearrange("p (b m j) -> p b j m", j=PACK, m=4)[:, :, slots, :],
            )

        for a in range(PASSES - 1):
            w_deal(a)
        nc.vector.tensor_copy(
            out=w_scales[:].rearrange("p (j m) -> p j m", j=PACK),
            in_=ws_raw[:].rearrange("p (m j) -> p j m", j=PACK),
        )

        x_grouped = [sbuf("x_grouped%d" % a, [P, T, PACK], BF16) for a in range(PASSES)]
        x_codes = [sbuf("x_codes%d" % a, [P, T], I32) for a in range(PASSES)]
        x_scales = [sbuf("x_scales%d" % a, [P, T], U8) for a in range(PASSES)]

        def x_copy(engine, a, cols):
            interleave(engine, x_grouped[a][:, cols, :], x_raw[a][:, :, cols])

        def x_quantize(a, cols):
            quantize(x_codes[a][:, cols], x_scales[a][:, cols], x_grouped[a][:, cols, :])

        def c_bank(h, j):
            return banks[PACK * h + j][:, half(0)]

        def down(a, h, slots=range(PACK)):
            cols = half(h)
            for j in slots:
                nc.tensor.matmul_mx(
                    out=c_bank(h, j),
                    lhsT=w_codes[a][:, j * P : (j + 1) * P].bitcast(FP8X4),
                    lhsT_scale=w_scales[4 * a : P, j * P : (j + 1) * P],
                    rhs=x_codes[a][:, cols].bitcast(FP8X4),
                    rhs_scale=x_scales[a][:, cols],
                    start=(a == 0),
                    stop=(a == PASSES - 1),
                )

        c_sb = sbuf("c_sb", [P, PACK, T], F32)
        c_grouped = sbuf("c_grouped", [P, T, PACK], BF16)
        c_codes = sbuf("c_codes", [P, T], I32)
        c_scales = sbuf("c_scales", [P, T], U8)

        def c_drain(engine, h, j):
            copy_on(engine, c_sb[:, j, half(h)], c_bank(h, j))

        def c_store(slots):
            nc.sync.dma_start(out=out_2.rearrange("(p j) t -> p j t", j=PACK)[:, slots, :], in_=c_sb[:, slots, :])

        def c_round(engine, cols):
            interleave(engine, c_grouped[:, cols, :], c_sb[:, :, cols])

        def c_quantize(cols):
            quantize(c_codes[:, cols], c_scales[:, cols], c_grouped[:, cols, :])

        def scales_store(row):
            nc.sync.dma_start(
                out=out_4[0, row : 16 : 4, :].bitcast(I32),
                in_=c_scales[row : P : 32, :].bitcast(I32),
            )

        wk_grouped = sbuf("wk_grouped", [P, M, PACK], BF16)
        wk_codes = sbuf("wk_codes", [P, M], I32)
        wk_scales = sbuf("wk_scales", [P, M], U8)
        kk_sb = [sbuf("kk_sb%d" % b, [P, T], F32) for b in range(4)]
        wv_grouped = [sbuf("wv_grouped%d" % h, [P, HALF, PACK], BF16) for h in range(2)]
        wv_codes = [sbuf("wv_codes%d" % h, [P, HALF], I32) for h in range(2)]
        wv_scales = [sbuf("wv_scales%d" % h, [P, HALF], U8) for h in range(2)]
        vv_sb = [sbuf("vv_sb%d" % h, [P, 2, T], F32) for h in range(2)]

        def wk_copy(engine, cols):
            interleave(engine, wk_grouped[:, cols, :], wk_raw[:, :, cols])

        def wk_quantize(cols):
            quantize(wk_codes[:, cols], wk_scales[:, cols], wk_grouped[:, cols, :])

        def wv_copy(engine, h):
            copy_on(
                engine,
                wv_grouped[h][:].rearrange("p (e b m) j -> p b j m e", e=2, m=2),
                wv_raw[:, :, half(h)].rearrange("p j (b m e) -> p b j m e", e=2, m=2),
            )

        def wv_quantize(h):
            quantize(wv_codes[h][:], wv_scales[h][:], wv_grouped[h][:])

        def up(bank, codes, scales, cols):
            nc.tensor.matmul_mx(
                out=bank[:, cols],
                lhsT=codes.bitcast(FP8X4),
                lhsT_scale=scales,
                rhs=c_codes[:, cols].bitcast(FP8X4),
                rhs_scale=c_scales[:, cols],
                start=True,
                stop=True,
            )

        def kk(b, cols=whole, bank=None):
            bank = banks[4 + b] if bank is None else bank
            up(bank, wk_codes[:, quarter(b)], wk_scales[:, quarter(b)], cols)

        vv_banks = [banks[3], banks[1], banks[4], banks[5]]

        def vv(h):
            for e in range(2):
                up(vv_banks[2 * h + e], wv_codes[h][:, e * P : (e + 1) * P], wv_scales[h][:, e * P : (e + 1) * P], whole)

        def warm_up(codes, scales):
            nc.tensor.matmul_mx(
                out=banks[7][:],
                lhsT=codes.bitcast(FP8X4),
                lhsT_scale=scales,
                rhs=x_codes[PASSES - 1][:].bitcast(FP8X4),
                rhs_scale=x_scales[PASSES - 1][:],
                start=True,
                stop=True,
            )

        def kk_drain(engine, b, cols=whole, bank=None):
            bank = banks[4 + b] if bank is None else bank
            copy_on(engine, kk_sb[b][:, cols], bank[:, cols])

        def kk_store(b):
            nc.sync.dma_start(out=out_0[quarter(b), :], in_=kk_sb[b][:])

        def vv_out(h):
            copy_on("scalar", vv_sb[h][:, 0, :], vv_banks[2 * h][:])
            copy_on("vector", vv_sb[h][:, 1, :], vv_banks[2 * h + 1][:])
            nc.sync.dma_start(out=out_1[half(h), :].rearrange("(p e) t -> p e t", e=2), in_=vv_sb[h][:])

        last = PASSES - 1
        for a in range(last):
            x_copy("vector", a, half(0))
            x_copy("scalar", a, half(1))
            for h in range(2):
                x_quantize(a, half(h))
                down(a, h)
        x_copy("vector", last, slice(0, 176))
        x_copy("scalar", last, slice(176, HALF))
        x_copy("vector", last, slice(400, T))
        x_copy("scalar", last, slice(HALF, 400))
        w_deal(last, slice(0, 2))
        x_quantize(last, half(0))
        w_deal(last, slice(2, 4))
        down(last, 0)
        x_quantize(last, half(1))
        down(last, 1)
        for h in range(2):
            for j in range(PACK):
                c_drain("scalar" if j % 2 == 0 else "vector", h, j)
        c_store(slice(0, PACK))
        for n in range(2):
            warm_up(w_codes[last][:, quarter(n)], w_scales[4 * last : P, quarter(n)])
        wk_copy("scalar", quarter(0))
        wk_copy("vector", quarter(1))
        c_round("scalar", slice(352, T))
        c_round("vector", slice(0, 352))
        wk_quantize(half(0))
        c_quantize(half(0))
        kk(0, half(0))
        kk(1, half(0))
        c_quantize(half(1))
        kk(0, half(1), banks[0])
        kk(1, half(1), banks[1])
        nc.sync.dma_start(out=out_3[0].rearrange("p t i -> p (t i)").bitcast(I32), in_=c_codes[:])
        for row in range(4):
            scales_store(row)
        wk_copy("scalar", quarter(2))
        wk_copy("scalar", quarter(3))
        wk_quantize(quarter(2))
        kk(2)
        wv_copy("vector", 0)
        wk_quantize(quarter(3))
        kk(3)
        for b in range(2):
            kk_drain("scalar", b, half(0))
            kk_drain("scalar", b, half(1), banks[b])
            kk_store(b)
        wv_quantize(0)
        vv(0)
        wv_copy("vector", 1)
        for b in (2, 3):
            kk_drain("scalar", b)
            kk_store(b)
        wv_quantize(1)
        vv(1)
        for h in range(2):
            vv_out(h)
